import numpy as np
import ml_dtypes


def mxq(x, axis, fmt="e4m3"):
    dtype, down = {"e4m3": (ml_dtypes.float8_e4m3fn, 7), "e5m2": (ml_dtypes.float8_e5m2, 14)}[fmt]
    v = np.moveaxis(np.asarray(x, np.float32).astype(ml_dtypes.bfloat16).astype(np.float64), axis, -1)
    blocks = v.reshape(v.shape[:-1] + (-1, 32))
    amax = np.abs(blocks).max(-1, keepdims=True)
    byte = np.maximum(np.where(amax > 0, np.frexp(amax)[1] - 1 + 127, 0) - down, 1)
    scale = np.exp2(byte - 127.0)
    codes = (blocks / scale).astype(np.float32).astype(dtype).astype(np.float64)
    return np.moveaxis((codes * scale).reshape(v.shape), -1, axis)


WIDE = False


def mx_kscale(k, group=512):
    if not WIDE:
        return np.ones(k)
    levels = np.array([10, -10, 5, -5, 0])
    if group != 512:
        return np.exp2(np.random.permutation(np.resize(levels, k // group))).repeat(group)
    if k % 512:
        return np.exp2(np.random.permutation(np.resize(levels, k // 32))).repeat(32)
    a = np.empty((k // 512, 16))
    for p in range(k // 512):
        a[p, :8] = np.random.permutation(np.resize(levels, 8))
        for g in range(8):
            far = levels[np.abs(levels - a[p, g]) >= 10]
            a[p, g + 8] = far[np.random.randint(len(far))]
    return np.exp2(a.ravel()).repeat(32)


def f64(x):
    return np.asarray(x).astype(np.float64)


def striped(idx):
    return np.tile(np.asarray(idx).reshape(-1, 16).T, (8, 1)).astype(np.uint16)


def unstriped(offs):
    return offs[:16].T.reshape(-1).astype(np.int64)


H, KV, D, NQ, N = 4, 2, 256, 512, 512
CAP = 2.0


def setup_inputs():
    n = np.random.standard_normal
    s = mx_kscale(D, 0)[:, None]
    u = mx_kscale(N)
    t = np.random.uniform(0.5, 2.0, N) * u
    v = n((KV, N, 128))
    return {
        "qT": (n((H, D, NQ)) * s * (0.70 / np.sqrt(D))).astype(np.float32),
        "kT": (n((KV, D, N)) / s).astype(np.float32),
        "t": t.reshape(N, 1).astype(np.float32),
        "v": (v / t[:, None]).astype(np.float32),
        "gn": np.tile(np.random.uniform(0.5, 2.0, 128), (128, 1)).astype(np.float32),
        "og": n((H, NQ, 128)).astype(np.float32),
    }


def reference(qT, kT, t, v, gn, og):
    a = np.repeat(mxq(f64(kT), 1, "e4m3"), H // KV, 0).transpose(0, 2, 1) @ mxq(f64(qT), 1, "e4m3")
    a = CAP * np.tanh(a / CAP)
    p = a / (1.0 + np.exp(-a))
    w = p * f64(t)
    y = mxq(w, 1, "e4m3").transpose(0, 2, 1) @ np.repeat(mxq(f64(v), 1, "e4m3"), H // KV, 0)
    y = y / 16.0
    y = y / np.sqrt(np.mean(np.square(y), -1, keepdims=True) + 1e-5) * f64(gn)[:1]
    y = y / (1.0 + np.exp(-f64(og)))
    return y

import math
from contextlib import ExitStack

import concourse.mybir as mybir

F32 = mybir.dt.float32
BF16 = mybir.dt.bfloat16
I32 = mybir.dt.int32
U32 = mybir.dt.uint32
U8 = mybir.dt.uint8
FP8X4 = mybir.dt.float8_e4m3fn_x4
ACT = mybir.ActivationFunctionType
ALU = mybir.AluOpType

H, KV, D, NQ, N, E = 4, 2, 256, 512, 512, 128
CAP = 2.0
EPS = 1e-5
P = 128
ROWS = 64
PACK = 4
QT = 128
PAIRS = 8
FLOPS = 2 * H * N * NQ * D + 2 * H * NQ * N * E

Q_LOADS = [(0, 1), (1, 2), (2, 4)]
K_SPLIT = 104
GROUPS = [(0, 1, 2, 3), (4, 5), (6,), (7,)]
PAIR = [(0, 0), (0, 1), (1, 0), (1, 1), (0, 2), (1, 2), (0, 3), (1, 3)]
SUM_EPS = E * 256.0 * EPS
ORDER = [
    ("load_k", 0),
    ("consts",),
    ("load_k", 1),
    ("load_q", 1, 0),
    ("load_q", 0, 0),
    ("load_og", 0),
    ("load_og", 1),
    ("load_t",),
    ("load_q", 1, 1),
    ("first_act",),
    ("load_gn",),
    ("cast_k", 0, 64, True),
    ("quant_k", 0, 0),
    ("quant_k", 0, 3),
    ("load_q", 0, 1),
    ("cast_k", 104, 128, False),
    ("quant_k", 0, 2),
    ("cast_k", 64, 104, True),
    ("load_og", 3),
    ("cast_q", 1, 0, 1, True),
    ("quant_k", 1, 1),
    ("quant_k", 1, 2),
    ("load_og", 2),
    ("cast_q", 0, 0, 1, False),
    ("quant_k", 1, 0),
    ("quant_k", 1, 3),
    ("quant_q", 1, 0, 1),
    ("quant_k", 0, 1),
    ("load_q", 1, 2),
    ("gate", 0, 1),
    ("scores", 0, 1),
    ("quant_q", 0, 0, 1),
    ("load_q", 0, 2),
    ("swap_k", 0),
    ("gate", 1, 2),
    ("scores", 0, 0),
    ("load_v",),
    ("cast_q", 1, 1, 2, True),
    ("cap", 0, 1),
    ("scale_gn",),
    ("swap_k", 1),
    ("quant_q", 1, 1, 2),
    ("cap", 0, 0),
    ("cast_q", 0, 1, 2, True),
    ("scores", 1, 1),
    ("make_gain", 1, 2),
    ("silu", 0, 2, 4),
    ("quant_q", 0, 1, 2),
    ("silu", 0, 0, 2),
    ("weigh", 0, 2, 4),
    ("scores", 1, 0),
    ("cap", 1, 1),
    ("weigh", 0, 0, 2),
    ("scores", 2),
    ("gate", 2, 4),
    ("cast_q", 1, 2, 4, True),
    ("cap", 1, 0),
    ("scores", 3),
    ("cast_q", 0, 2, 4, True),
    ("cap", 2, 1),
    ("quant_q", 1, 2, 4),
    ("cap", 2, 0),
    ("quant_q", 0, 2, 4),
    ("silu", 1),
    ("cast_v",),
    ("scores", 4),
    ("silu", 2),
    ("weigh", 1),
    ("cap", 3, 1),
    ("quant_v",),
    ("cap", 3, 0),
    ("quant_w", 1),
    ("quant_w", 0),
    ("cap", 4, 1),
    ("second", 1, 0),
    ("weigh", 2),
    ("second", 1, 1),
    ("second", 0, 1),
    ("silu", 3),
    ("scores", 5),
    ("make_gain", 2, 4),
    ("cap", 4, 0),
    ("weigh", 3),
    ("cap", 5, 0),
    ("scores", 6),
    ("silu", 4),
    ("quant_w", 2),
    ("bn", 1),
    ("cap", 5, 1),
    ("quant_w", 3),
    ("second", 0, 0),
    ("weigh", 4),
    ("cap", 6, 0),
    ("second", 3, 0),
    ("second", 2, 1),
    ("second", 3, 1),
    ("cap", 6, 1),
    ("second", 2, 0),
    ("scores", 7),
    ("bn", 0),
    ("silu", 5),
    ("bn", 2),
    ("bn", 3),
    ("mean_sq", 0),
    ("silu", 6),
    ("quant_w", 4),
    ("weigh", 5),
    ("cap", 7, 0),
    ("weigh", 6),
    ("cap", 7, 1),
    ("silu", 7, 0, 2),
    ("quant_w", 5),
    ("silu", 7, 2, 4),
    ("quant_w", 6),
    ("weigh", 7, 0, 2),
    ("second", 6, 0),
    ("second", 5, 1),
    ("weigh", 7, 2, 4),
    ("second", 4, 1),
    ("second", 5, 0),
    ("second", 4, 0),
    ("quant_w", 7, 0, 2),
    ("denom", 0),
    ("quant_w", 7, 2, 4),
    ("second", 7, 0),
    ("make_gain", 0, 1),
    ("root", 0),
    ("second", 7, 1),
    ("square", 4, 1),
    ("second", 6, 1),
    ("square", 5, 1),
    ("finish", 3, 0),
    ("finish", 3, 1),
    ("square", 5, 0),
    ("finish", 1, 1),
    ("square", 4, 0),
    ("finish", 2, 1),
    ("store", 3),
    ("square", 6, 0),
    ("finish", 1, 0),
    ("square", 7, 1),
    ("finish", 2, 0),
    ("finish", 0, 1),
    ("root_of_sum", 1, 0, 4),
    ("store", 1),
    ("square", 6, 1),
    ("finish", 0, 0),
    ("store", 2),
    ("square", 7, 0),
    ("finish", 4, 0),
    ("finish", 4, 1),
    ("root_of_sum", 2, 0, 2),
    ("store", 0),
    ("root_of_sum", 3, 1, 2),
    ("finish", 5, 1),
    ("root_of_sum", 3, 0, 1),
    ("finish", 5, 0),
    ("store", 4),
    ("finish", 6, 0),
    ("finish", 6, 1),
    ("store", 5),
    ("finish", 7, 0),
    ("finish", 7, 1),
    ("store", 6),
    ("store", 7),
]


def tile_rows_a_silu_cap_onorm_gate_kernel(tc, qT, kT, t, v, gn, og, out):
    nc = tc.nc
    with ExitStack() as ctx:
        sb = ctx.enter_context(tc.tile_pool(name="sb", bufs=1))
        ps = ctx.enter_context(tc.psum_pool(name="ps", bufs=1))

        def tile(shape, dtype, name):
            return sb.tile(shape, dtype, name=name, align_bytes=64)

        k_raw = [tile([P, PACK, N // 2], F32, "k_raw%d" % i) for i in range(2)]
        k_bf = tile([P, PACK, P, PACK], BF16, "k_bf")
        k_mx = [tile([P, N + N // 4], I32, "k_mx%d" % i) for i in range(2)]
        k_codes = [x[:, :N] for x in k_mx]
        k_scales = [x[:, N:].bitcast(U8) for x in k_mx]
        q_raw = [[tile([P, PACK, QT * (b - a)], F32, "q_raw%d_%d" % (u, a)) for a, b in Q_LOADS] for u in range(2)]
        q_bf = [tile([P, NQ, PACK], BF16, "q_bf%d" % u) for u in range(2)]
        q_codes = [tile([P, NQ], U32, "q_codes%d" % u) for u in range(2)]
        q_scales = [tile([P, NQ], U8, "q_scales%d" % u) for u in range(2)]
        v_raw = tile([P, KV, PACK, E], F32, "v_raw")
        v_bf = tile([P, KV, E, PACK], BF16, "v_bf")
        v_codes = tile([P, KV * E], U32, "v_codes")
        v_scales = tile([P, KV * E], U8, "v_scales")
        t_sb = tile([P, PACK], F32, "t_sb")
        gn_sb = tile([P, E], F32, "gn_sb")
        gn_half = tile([P, E], F32, "gn_half")
        og_sb = tile([P, 4 * H, E], F32, "og_sb")
        gate_t = tile([P, 4 * H, E], F32, "gate_t")
        gain = tile([P, 4 * H, E], F32, "gain")
        th = [tile([P, KV, QT, PACK], F32, "th%d" % i) for i in range(PAIRS)]
        pw = [tile([P, KV, QT, PACK], F32, "pw%d" % i) for i in range(PAIRS)]
        w_bf = [tile([P, KV, QT, PACK], BF16, "w_bf%d" % i) for i in range(PAIRS)]
        w_codes = [tile([P, KV * QT], U32, "w_codes%d" % i) for i in range(PAIRS)]
        w_scales = [tile([P, KV * QT], U8, "w_scales%d" % i) for i in range(PAIRS)]
        stats = [tile([P, 2 * len(m), 3], F32, "stats%d" % i) for i, m in enumerate(GROUPS)]
        msq = [tile([P, 2 * len(m)], F32, "msq%d" % i) for i, m in enumerate(GROUPS)]
        den = [tile([P, 2 * len(m)], F32, "den%d" % i) for i, m in enumerate(GROUPS)]
        rstd = [tile([P, 2 * len(m)], F32, "rstd%d" % i) for i, m in enumerate(GROUPS)]
        junk = tile([P, 2 * PAIRS, E], F32, "junk")
        zero = tile([P, 1], F32, "zero")
        zero_b = tile([P, 1], F32, "zero_b")
        o_sb = [tile([P, KV, E], F32, "o_sb%d" % i) for i in range(PAIRS)]

        sc = [[ps.tile([P, PACK, QT], F32, name="sc%d_%d" % (g, b)) for b in range(2)] for g in range(KV)]
        y = [ps.tile([P, 4, E], F32, name="y%d" % b) for b in range(4)]

        def head(n, a):
            return ((0, 3), (1, 2))[PAIR[n][0]][a]

        def y_of(n, a):
            return y[n // 2][:, 2 * (n % 2) + a, :]

        def pair_heads(x, i):
            return x[0:4:3] if i == 0 else x[1:3]

        def load_k(i):
            src = kT.rearrange("g (p j) n -> (g p) j n", j=PACK)
            nc.sync.dma_start(out=k_raw[i][:], in_=src[:, :, i * 256 : (i + 1) * 256])

        def load_q(u, c):
            a, b = Q_LOADS[c]
            src = qT[2 * u : 2 * u + 2].rearrange("h (p j) q -> (h p) j q", j=PACK)
            nc.sync.dma_start(out=q_raw[u][c][:], in_=src[:, :, a * QT : b * QT])

        def rows_of(x, n):
            i, qt = PAIR[n]
            return pair_heads(x, i).rearrange("a q e -> q a e")[qt * QT : (qt + 1) * QT]

        def load_og(qt):
            nc.sync.dma_start(out=og_sb[:, H * qt : H * (qt + 1)], in_=og.rearrange("h q e -> q h e")[qt * QT : (qt + 1) * QT])

        def swap_k(g):
            nc.scalar.dma_start(out=k_mx[1][ROWS * (1 - g) : ROWS * (2 - g)], in_=k_mx[0][ROWS * g : ROWS * (g + 1)])

        def copy(on_vector, dst, src):
            if on_vector:
                nc.vector.tensor_copy(out=dst, in_=src)
            else:
                nc.scalar.copy(out=dst, in_=src)

        def cast_k(s0, s1, on_vector):
            i = s0 // 64
            copy(
                on_vector,
                k_bf[:, :, s0:s1, :].rearrange("p r s j -> p s r j"),
                k_raw[i][:].rearrange("p j (s r) -> p s r j", r=PACK)[:, s0 - 64 * i : s1 - 64 * i],
            )

        def quant_k(i, r):
            cols = slice(r * P + 64 * i, r * P + 64 * (i + 1))
            nc.vector.quantize_mx(
                out=k_codes[0][:, cols].bitcast(FP8X4),
                scales=k_scales[0][:, cols],
                in_=k_bf[:, r, 64 * i : 64 * (i + 1), :].rearrange("p s j -> p (s j)"),
            )

        def cast_q(u, a, b, on_vector):
            c = [i for i, (lo, hi) in enumerate(Q_LOADS) if lo <= a < hi][0]
            lo = Q_LOADS[c][0]
            copy(
                on_vector,
                q_bf[u][:, a * QT : b * QT, :].rearrange("p (c i) j -> p c j i", i=4),
                q_raw[u][c][:, :, (a - lo) * QT : (b - lo) * QT].rearrange("p j (c i) -> p c j i", i=4),
            )

        def quant_q(u, a, b):
            cols = slice(a * QT, b * QT)
            nc.vector.quantize_mx(
                out=q_codes[u][:, cols].bitcast(FP8X4),
                scales=q_scales[u][:, cols],
                in_=q_bf[u][:, cols, :].rearrange("p q j -> p (q j)"),
            )

        def cast_v():
            nc.vector.tensor_copy(
                out=v_bf[:].rearrange("p g (c i) r -> p g c r i", i=4),
                in_=v_raw[:].rearrange("p g r (c i) -> p g c r i", i=4),
            )

        def quant_v():
            nc.vector.quantize_mx(
                out=v_codes[:].bitcast(FP8X4), scales=v_scales[:], in_=v_bf[:].rearrange("p g e r -> p (g e r)")
            )

        def scores(n, only=None):
            i, qt = PAIR[n]
            cols = slice(qt * QT, (qt + 1) * QT)
            for r in range(PACK):
                for a in range(KV) if only is None else (only,):
                    h = head(n, a)
                    g = h % 2
                    rows = slice(ROWS * g, ROWS * (g + 1))
                    nc.tensor.matmul_mx(
                        out=sc[g][n % 2][:, r, :],
                        lhsT=k_codes[i][rows, r * P : (r + 1) * P].bitcast(FP8X4),
                        lhsT_scale=k_scales[i][rows, r * P : (r + 1) * P],
                        rhs=q_codes[h // 2][rows, cols].bitcast(FP8X4),
                        rhs_scale=q_scales[h // 2][rows, cols],
                        start=True,
                        stop=True,
                    )

        def cap(n, a):
            src = sc[head(n, a) % 2][n % 2][:].rearrange("p r q -> p q r")
            nc.scalar.activation(out=th[n][:, a], in_=src, func=ACT.Tanh, scale=1.0 / CAP)

        def flat(x, a, b):
            return x[:].rearrange("p g q r -> p (g q) r")[:, 64 * a : 64 * b, :]

        def silu(n, a=0, b=4):
            nc.scalar.activation(out=flat(pw[n], a, b), in_=flat(th[n], a, b), func=ACT.Silu, scale=CAP)

        def weigh(n, a=0, b=4):
            nc.vector.tensor_tensor(
                out=flat(w_bf[n], a, b),
                in0=flat(pw[n], a, b),
                in1=t_sb[:].unsqueeze(1).broadcast_to([P, 64 * (b - a), PACK]),
                op=ALU.mult,
            )

        def quant_w(n, a=0, b=4):
            nc.vector.quantize_mx(
                out=w_codes[n][:, 64 * a : 64 * b].bitcast(FP8X4),
                scales=w_scales[n][:, 64 * a : 64 * b],
                in_=flat(w_bf[n], a, b).rearrange("p q r -> p (q r)"),
            )

        def second(n, a):
            nc.tensor.matmul_mx(
                out=y_of(n, a),
                lhsT=w_codes[n][:, a * QT : (a + 1) * QT].bitcast(FP8X4),
                lhsT_scale=w_scales[n][:, a * QT : (a + 1) * QT],
                rhs=v_codes[:, a * E : (a + 1) * E].bitcast(FP8X4),
                rhs_scale=v_scales[:, a * E : (a + 1) * E],
                start=True,
                stop=True,
            )

        def gate(a, b):
            bias = zero_b[:] if a == 0 else 0.0
            nc.scalar.activation(
                out=gate_t[:, H * a : H * b], in_=og_sb[:, H * a : H * b], func=ACT.Tanh, scale=0.5, bias=bias
            )

        def make_gain(a, b):
            nc.vector.scalar_tensor_tensor(
                out=gain[:, H * a : H * b],
                in0=gate_t[:, H * a : H * b],
                scalar=1.0,
                in1=gn_half[:].unsqueeze(1).broadcast_to([P, H * (b - a), E]),
                op0=ALU.add,
                op1=ALU.mult,
            )

        def group_of(n):
            grp = [i for i, m in enumerate(GROUPS) if n in m][0]
            return grp, 2 * GROUPS[grp].index(n)

        def bn(n):
            grp, c = group_of(n)
            b = 2 * (n % 2)
            nc.vector.bn_stats(
                out=stats[grp][:, c : c + 2, :].rearrange("p a s -> p (a s)"),
                in_=y[n // 2][:, b : b + 2, :].rearrange("p a e -> p e a"),
            )

        def mean_sq(grp):
            nc.vector.scalar_tensor_tensor(
                out=msq[grp][:], in0=stats[grp][:, :, 1], scalar=float(E), in1=stats[grp][:, :, 1],
                op0=ALU.mult, op1=ALU.mult,
            )

        def denom(grp):
            nc.vector.scalar_tensor_tensor(
                out=den[grp][:], in0=stats[grp][:, :, 2], scalar=SUM_EPS, in1=msq[grp][:], op0=ALU.add, op1=ALU.add
            )

        def root(grp):
            nc.scalar.activation(out=rstd[grp][:], in_=den[grp][:], func=ACT.Abs_reciprocal_sqrt)

        def square(n, a):
            grp, c = group_of(n)
            nc.scalar.activation(
                out=junk[:, 2 * n + a], in_=y_of(n, a), func=ACT.Square, accum_out=msq[grp][:, c + a : c + a + 1]
            )

        def root_of_sum(grp, a, b):
            nc.scalar.activation(out=rstd[grp][:, a:b], in_=msq[grp][:, a:b], func=ACT.Abs_reciprocal_sqrt, bias=SUM_EPS)

        def finish(n, a):
            grp, c = group_of(n)
            nc.vector.scalar_tensor_tensor(
                out=o_sb[n][:, a, :], in0=y_of(n, a), scalar=rstd[grp][:, c + a : c + a + 1],
                in1=gain[:, H * PAIR[n][1] + head(n, a), :], op0=ALU.mult, op1=ALU.mult,
            )

        def store(n, a=0, b=2):
            nc.sync.dma_start(out=rows_of(out, n)[:, a:b], in_=o_sb[n][:, a:b])

        def load_t():
            nc.sync.dma_start(out=t_sb[:], in_=t.rearrange("(s r) o -> s (r o)", r=PACK))

        def load_v():
            nc.sync.dma_start(out=v_raw[:], in_=v.rearrange("g (s r) e -> s g r e", r=PACK))

        def load_gn():
            nc.sync.dma_start(out=gn_sb[:], in_=gn)

        def consts():
            nc.gpsimd.memset(zero[:], 0.0)
            nc.gpsimd.memset(k_mx[0][:, N:], 0)

        def first_act():
            nc.scalar.activation(out=zero_b[:], in_=zero[:], func=ACT.Silu)

        def scale_gn():
            nc.vector.tensor_scalar(
                out=gn_half[:], in0=gn_sb[:], scalar1=0.5 * math.sqrt(E), scalar2=None, op0=ALU.mult
            )

        steps = {
            "load_k": load_k, "load_q": load_q, "load_og": load_og, "cast_k": cast_k, "quant_k": quant_k,
            "cast_q": cast_q, "quant_q": quant_q, "cast_v": cast_v, "quant_v": quant_v, "scores": scores,
            "cap": cap, "silu": silu, "weigh": weigh, "quant_w": quant_w, "second": second, "gate": gate,
            "make_gain": make_gain, "bn": bn, "mean_sq": mean_sq, "root": root, "denom": denom, "square": square,
            "finish": finish, "store": store, "load_t": load_t, "load_v": load_v, "swap_k": swap_k,
            "load_gn": load_gn, "consts": consts, "first_act": first_act, "scale_gn": scale_gn,
            "root_of_sum": root_of_sum,
        }

        ctx.enter_context(tc.manual_schedule())
        for step in ORDER:
            steps[step[0]](*step[1:])
